import numpy as np
import ml_dtypes


def mxq(x, axis, fmt="e4m3"):
    dtype, down = {"e4m3": (ml_dtypes.float8_e4m3fn, 7), "e5m2": (ml_dtypes.float8_e5m2, 14)}[fmt]
    v = np.moveaxis(np.asarray(x, np.float32).astype(ml_dtypes.bfloat16).astype(np.float64), axis, -1)
    blocks = v.reshape(v.shape[:-1] + (-1, 32))
    amax = np.abs(blocks).max(-1, keepdims=True)
    byte = np.maximum(np.where(amax > 0, np.frexp(amax)[1] - 1 + 127, 0) - down, 1)
    scale = np.exp2(byte - 127.0)
    codes = (blocks / scale).astype(np.float32).astype(dtype).astype(np.float64)
    return np.moveaxis((codes * scale).reshape(v.shape), -1, axis)


WIDE = False


def mx_kscale(k):
    if not WIDE:
        return np.ones(k)
    levels = np.array([30, -30])
    if k % 512:
        return np.exp2(np.random.permutation(np.resize(levels, k // 32))).repeat(32)
    a = np.empty((k // 512, 16))
    for p in range(k // 512):
        a[p, :8] = np.random.permutation(np.resize(levels, 8))
        for g in range(8):
            far = levels[np.abs(levels - a[p, g]) >= 10]
            a[p, g + 8] = far[np.random.randint(len(far))]
    return np.exp2(a.ravel()).repeat(32)


def f64(x):
    return np.asarray(x).astype(np.float64)


def striped(idx):
    return np.tile(np.asarray(idx).reshape(-1, 16).T, (8, 1)).astype(np.uint16)


def unstriped(offs):
    return offs[:16].T.reshape(-1).astype(np.int64)


K, J, N, T, V = 256, 1024, 256, 2048, 2048


def setup_inputs():
    n = np.random.standard_normal
    idx = np.random.permutation(T)[:J]
    idx2 = np.random.permutation(V)[:J]
    fj = mx_kscale(J)
    return {
        "xf": (n((K, T))).astype(np.float32),
        "ra": (np.random.uniform(0.5, 1.5, (1, J)) * fj).astype(np.float32),
        "gt": (n((N, V)) * np.exp(0.5 * n((1, V)))).astype(np.float32),
        "rb": (np.random.uniform(0.5, 1.5, (1, J)) / fj).astype(np.float32),
        "gk": (np.random.uniform(0.5, 2.0, (K, 1))).astype(np.float32),
        "bn": (np.random.uniform(-12.0, 12.0, (1, N))).astype(np.float32),
        "offs": striped(idx),
        "offs2": striped(idx2),
    }


def reference(xf, ra, gt, rb, gk, bn, offs, offs2):
    idx = unstriped(offs)
    idx2 = unstriped(offs2)
    xg = f64(xf)[:, idx]
    x1 = np.pad(xg, ((0, 0), (1, 0)))[:, :J]
    us = (xg - 0.6 * x1) * f64(ra)
    uj = us.T
    gs = f64(gt)[:, idx2] * f64(rb)
    gj = gs.T
    ujq = mxq(uj, 0, "e4m3")
    gjq = mxq(gj, 0, "e5m2")
    w = ujq.T @ gjq
    wb = w + f64(bn)
    mn = np.mean(wb, axis=1, keepdims=True)
    dw = wb - mn
    y = dw / (np.mean(np.abs(dw), axis=1, keepdims=True) + 2.0) * f64(gk)
    return y

@@ -1,0 +1,242 @@
+from contextlib import ExitStack
+
+import concourse.mybir as mybir
+from concourse.masks import make_identity
+
+K, J, N, T = 256, 1024, 256, 2048
+FLOPS = 2 * K * J * N
+
+F32 = mybir.dt.float32
+BF16 = mybir.dt.bfloat16
+U32 = mybir.dt.uint32
+U16 = mybir.dt.uint16
+U8 = mybir.dt.uint8
+E4M3 = mybir.dt.float8_e4m3fn_x4
+E5M2 = mybir.dt.float8_e5m2_x4
+ALU = mybir.AluOpType
+ACT = mybir.ActivationFunctionType
+
+P = 128
+PACK = 4
+PASS = P * PACK
+PASSES = J // PASS
+HALVES = 2
+PER_COL = 16
+LEAD = 8
+
+
+def tile_list_moment_steps_listed_spread_kernel(tc, xf, ra, gt, rb, gk, bn, offs, offs2, out):
+    nc = tc.nc
+    with ExitStack() as ctx:
+        keep = ctx.enter_context(tc.tile_pool(name="keep", bufs=1))
+        psum = ctx.enter_context(tc.psum_pool(name="psum", bufs=1))
+
+        def reused(shape, dtype, name, tag):
+            return keep.tile(shape, dtype, name=name, tag=tag, align_bytes=64)
+
+        x_list = keep.tile([P, J // PER_COL], U16, name="x_list")
+        g_list = keep.tile([P, J // PER_COL], U16, name="g_list")
+        x_tab = [keep.tile([P, T], F32, name=f"x_tab{h}") for h in range(HALVES)]
+        g_tab = [keep.tile([P, T], F32, name=f"g_tab{h}") for h in range(HALVES)]
+        ra_col = keep.tile([P, PASSES, PACK], F32, name="ra_col")
+        rb_col = reused([P, PASSES, PACK], F32, "rb_col", "first")
+        bn_col = keep.tile([P, 2], F32, name="bn_col")
+        gk_col = keep.tile([P, HALVES], F32, name="gk_col")
+
+        xf_rows = xf.rearrange("(p h) t -> p h t", h=HALVES)
+        out_rows = out.rearrange("(p h) n -> p h n", h=HALVES)
+        nc.sync.dma_start(rb_col[:], rb.rearrange("o (a p t) -> p (o a) t", p=P, t=PACK))
+        nc.sync.dma_start(x_tab[0][:], xf_rows[:, 0, :])
+        nc.sync.dma_start(x_list[:], offs)
+        nc.sync.dma_start(ra_col[:], ra.rearrange("o (a p t) -> p (o a) t", p=P, t=PACK))
+        nc.sync.dma_start(bn_col[:], bn.rearrange("o (p c) -> p (o c)", c=2))
+        nc.sync.dma_start(x_tab[1][:], xf_rows[:, 1, :])
+        nc.sync.dma_start(g_list[:], offs2)
+        nc.sync.dma_start(g_tab[0][:], gt[0:P, :])
+        nc.sync.dma_start(g_tab[1][:], gt[P : 2 * P, :])
+        nc.sync.dma_start(gk_col[:], gk.rearrange("(p h) o -> p (h o)", h=HALVES))
+
+        zero = keep.tile([P, 1], F32, name="zero")
+        nc.gpsimd.memset(zero[:], 0.0)
+        ident = keep.tile([P, P], F32, name="ident")
+        make_identity(nc, ident[:])
+
+        def turn_bank():
+            return psum.tile([P, PACK, P], F32, name="turn", tag="turn", bufs=3)
+
+        x_pick = [reused([P, LEAD + J], F32, "x_pick0", "x_pick0")]
+        nc.scalar.activation(x_pick[0][:, LEAD - 1 : LEAD], zero[:], ACT.Copy)
+
+        def gather(on_vector, dst, table, entries, first, count):
+            window = table[:].indirect(entries[:, first // PER_COL : (first + count) // PER_COL])
+            if on_vector:
+                nc.vector.tensor_copy(dst, window)
+            else:
+                nc.scalar.activation(dst, window, ACT.Copy)
+
+        def x_gather(on_vector, h, a):
+            first = LEAD + a * PASS
+            gather(on_vector, x_pick[h][:, first : first + PASS], x_tab[h], x_list, a * PASS, PASS)
+
+        u_codes = [keep.tile([P, PASSES * P], U32, name=f"u_codes{h}", align_bytes=64) for h in range(HALVES)]
+        u_scales = [keep.tile([P, PASSES * P], U8, name=f"u_scales{h}", align_bytes=64) for h in range(HALVES)]
+        g_codes = [keep.tile([P, PASSES * P], U32, name=f"g_codes{h}", align_bytes=64) for h in range(HALVES)]
+        g_scales = [keep.tile([P, PASSES * P], U8, name=f"g_scales{h}", align_bytes=64) for h in range(HALVES)]
+
+        def x_step(h, a, step):
+            first = LEAD + a * PASS
+            nc.vector.scalar_tensor_tensor(
+                step[:].rearrange("p (t q) -> p q t", t=PACK),
+                x_pick[h][:, first - 1 : first - 1 + PASS].rearrange("p (q t) -> p q t", t=PACK),
+                -0.6,
+                x_pick[h][:, first : first + PASS].rearrange("p (q t) -> p q t", t=PACK),
+                ALU.mult,
+                ALU.add,
+            )
+            bank = turn_bank()
+            for t in range(PACK):
+                nc.tensor.transpose(bank[:, t, :], step[:, t * P : (t + 1) * P], ident[:])
+            return bank
+
+        def x_weigh(a, bank, u_bf):
+            nc.vector.tensor_tensor(
+                u_bf[:].rearrange("p (k t) -> p k t", t=PACK),
+                bank[:].rearrange("p t k -> p k t"),
+                ra_col[:, a, :].unsqueeze(1).to_broadcast([P, P, PACK]),
+                ALU.mult,
+            )
+
+        def x_quantise(h, a, u_bf):
+            cols = slice(a * P, (a + 1) * P)
+            nc.vector.quantize_mx(u_codes[h][:, cols].bitcast(E4M3), u_scales[h][:, cols], u_bf[:])
+
+        def g_weigh(picked, weighed, a):
+            nc.vector.tensor_tensor(
+                weighed.rearrange("p (u q e) -> p q u e", u=2, e=2),
+                picked.rearrange("p (q u e) -> p q u e", u=2, e=2),
+                rb_all[:, a * PASS : (a + 1) * PASS].rearrange("p (q u e) -> p q u e", u=2, e=2),
+                ALU.mult,
+            )
+
+        def g_turn(weighed, pairs_bank):
+            words = weighed.bitcast(F32)
+            for u in range(2):
+                nc.tensor.transpose(pairs_bank[:, u, :], words[:, u * P : (u + 1) * P], ident[:])
+
+        x_gather(True, 0, 0)
+        x_gather(False, 0, 1)
+        rb_all = keep.tile([P, J], F32, name="rb_all")
+        for a in range(PASSES):
+            bank = turn_bank()
+            for t in range(PACK):
+                nc.tensor.transpose(bank[:, t, :], rb_col[:, a, t : t + 1].to_broadcast([P, P]), ident[:])
+            nc.scalar.copy(
+                rb_all[:, a * PASS : (a + 1) * PASS].rearrange("p (q t) -> p q t", t=PACK),
+                bank[:].rearrange("p t q -> p q t"),
+            )
+
+        steps = [reused([P, PASS], F32, f"step0{a}", f"g0_pick{a}") for a in range(PASSES)]
+        banks = [x_step(0, a, steps[a]) for a in range(PASSES)]
+        u_bf = [reused([P, PASS], BF16, f"u_bf0{a}", f"early{a}") for a in range(PASSES)]
+        for a in range(PASSES):
+            x_weigh(a, banks[a], u_bf[a])
+        for a in range(PASSES):
+            x_quantise(0, a, u_bf[a])
+        g1_banks = [psum.tile([P, 2, 2, P], F32, name=f"g1_bank{a}") for a in range(PASSES)]
+        for c in range(2):
+            nc.tensor.transpose(g1_banks[1][:, 1, c, :], bn_col[:, c : c + 1].to_broadcast([P, P]), ident[:])
+        x_pick.append(reused([P, LEAD + J], F32, "x_pick1", "first"))
+        nc.scalar.activation(x_pick[1][:, LEAD - 1 : LEAD], zero[:], ACT.Copy)
+        for a in range(PASSES):
+            x_gather(False, 1, a)
+        steps = [reused([P, PASS], F32, f"step1{a}", f"early{a}") for a in range(PASSES)]
+        banks = [x_step(1, a, steps[a]) for a in range(PASSES)]
+        u_bf = [reused([P, PASS], BF16, f"u_bf1{a}", f"late{a}") for a in range(PASSES)]
+        for a in range(PASSES):
+            x_weigh(a, banks[a], u_bf[a])
+        for a in range(PASSES):
+            x_quantise(1, a, u_bf[a])
+        g0_pick = [reused([P, PASS], F32, f"g0_pick{a}", f"g0_pick{a}") for a in range(PASSES)]
+        for a in range(PASSES):
+            gather(False, g0_pick[a][:], g_tab[0], g_list, a * PASS, PASS)
+        g1_pick0 = reused([P, PASS], F32, "g1_pick0", "x_pick0")
+        gather(False, g1_pick0[:], g_tab[1], g_list, 0, PASS)
+        g0_bf = reused([P, J], BF16, "g0_bf", "late0")
+        g_weigh(g0_pick[0][:], g0_bf[:, 0:PASS], 0)
+        g1_pick1 = reused([P, PASS], F32, "g1_pick1", "late1")
+        quarter = PASS // 2
+        gather(False, g1_pick1[:, quarter:PASS], g_tab[1], g_list, PASS + quarter, quarter)
+        gather(True, g1_pick1[:, 0:quarter], g_tab[1], g_list, PASS, quarter)
+        g_weigh(g0_pick[1][:], g0_bf[:, PASS:J], 1)
+        g0_bank = psum.tile([P, PASSES, 2, P], F32, name="g0_bank")
+        for a in range(PASSES):
+            g_turn(g0_bf[:, a * PASS : (a + 1) * PASS], g0_bank[:, a])
+        g1_bf0 = reused([P, PASS], BF16, "g1_bf0", "g0_pick0")
+        g_weigh(g1_pick0[:], g1_bf0[:], 0)
+        g_turn(g1_bf0[:], g1_banks[0][:, 0])
+        g1_bf1 = keep.tile([P, PASS], BF16, name="g1_bf1")
+        g_weigh(g1_pick1[:], g1_bf1[:], 1)
+        g_turn(g1_bf1[:], g1_banks[1][:, 0])
+
+        g0_in = keep.tile([P, PASSES * PASS], BF16, name="g0_in", align_bytes=64)
+        nc.scalar.copy(
+            g0_in[:].bitcast(F32).rearrange("p (a n u) -> p a n u", a=PASSES, u=2),
+            g0_bank[:].rearrange("p a u n -> p a n u"),
+        )
+        g1_in = [keep.tile([P, PASS], BF16, name=f"g1_in{a}", align_bytes=64) for a in range(PASSES)]
+        for a in range(PASSES):
+            nc.scalar.copy(
+                g1_in[a][:].bitcast(F32).rearrange("p (n u) -> p n u", u=2),
+                g1_banks[a][:, 0].rearrange("p u n -> p n u"),
+            )
+        bn_all = keep.tile([P, N], F32, name="bn_all")
+        nc.scalar.copy(bn_all[:].rearrange("p (q c) -> p q c", c=2), g1_banks[1][:, 1].rearrange("p c q -> p q c"))
+        nc.vector.quantize_mx(g_codes[0][:].bitcast(E5M2), g_scales[0][:], g0_in[:])
+        for a in range(PASSES):
+            cols = slice(a * P, (a + 1) * P)
+            nc.vector.quantize_mx(g_codes[1][:, cols].bitcast(E5M2), g_scales[1][:, cols], g1_in[a][:])
+
+        w = [psum.tile([P, N], F32, name=f"w{h}") for h in range(HALVES)]
+
+        def product(h, c, a):
+            cols = slice(a * P, (a + 1) * P)
+            nc.tensor.matmul_mx(
+                out=w[h][:, c * P : (c + 1) * P],
+                lhsT=u_codes[h][:, cols].bitcast(E4M3),
+                lhsT_scale=u_scales[h][:, cols],
+                rhs=g_codes[c][:, cols].bitcast(E5M2),
+                rhs_scale=g_scales[c][:, cols],
+                start=(a == 0),
+                stop=(a == PASSES - 1),
+            )
+
+        for h in range(HALVES):
+            for a in range(PASSES):
+                product(h, 0, a)
+        for a in range(PASSES):
+            for h in range(HALVES):
+                product(h, 1, a)
+
+        row_sum = keep.tile([P, HALVES], F32, name="row_sum")
+        abs_sum = keep.tile([P, HALVES], F32, name="abs_sum")
+        wb = [keep.tile([P, N], F32, name=f"wb{h}") for h in range(HALVES)]
+        for h in range(HALVES):
+            nc.vector.scalar_tensor_tensor(
+                wb[h][:], w[h][:], 1.0, bn_all[:], ALU.mult, ALU.add, accum_out=row_sum[:, h : h + 1]
+            )
+        dev = [keep.tile([P, N], F32, name=f"dev{h}") for h in range(HALVES)]
+        for h in range(HALVES):
+            size = keep.tile([P, N], F32, name=f"size{h}")
+            nc.scalar.activation(
+                size[:], wb[h][:], ACT.Abs, bias=row_sum[:, h : h + 1], scale=-float(N), accum_out=abs_sum[:, h : h + 1]
+            )
+            nc.vector.tensor_scalar(dev[h][:], wb[h][:], float(N), row_sum[:, h : h + 1], ALU.mult, ALU.subtract)
+        den = keep.tile([P, HALVES], F32, name="den")
+        inv = keep.tile([P, HALVES], F32, name="inv")
+        nc.vector.tensor_scalar(den[:], abs_sum[:], 1.0 / N, 2.0 * N, ALU.mult, ALU.add)
+        nc.vector.reciprocal(inv[:], den[:])
+        for h in range(HALVES):
+            y = keep.tile([P, N], F32, name=f"y{h}")
+            nc.vector.tensor_scalar(y[:], dev[h][:], inv[:, h : h + 1], gk_col[:, h : h + 1], ALU.mult, ALU.mult)
+            queue = nc.sync if h == 0 else nc.scalar
+            queue.dma_start(out_rows[:, h, :], y[:])

@@ -22,7 +22,7 @@ PASS = P * PACK
 PASSES = J // PASS
 HALVES = 2
 PER_COL = 16
-LEAD = 8
+LEAD = 2 * PER_COL
 
 
 def tile_list_moment_steps_listed_spread_kernel(tc, xf, ra, gt, rb, gk, bn, offs, offs2, out):
@@ -39,8 +39,8 @@ def tile_list_moment_steps_listed_spread_kernel(tc, xf, ra, gt, rb, gk, bn, offs
         x_tab = [keep.tile([P, T], F32, name=f"x_tab{h}") for h in range(HALVES)]
         g_tab = [keep.tile([P, T], F32, name=f"g_tab{h}") for h in range(HALVES)]
         ra_col = keep.tile([P, PASSES, PACK], F32, name="ra_col")
-        rb_col = reused([P, PASSES, PACK], F32, "rb_col", "first")
-        bn_col = keep.tile([P, 2], F32, name="bn_col")
+        rb_col = reused([P, PASSES, PACK], F32, "rb_col", "a")
+        bn_col = reused([P, 2], F32, "bn_col", "b")
         gk_col = keep.tile([P, HALVES], F32, name="gk_col")
 
         xf_rows = xf.rearrange("(p h) t -> p h t", h=HALVES)
@@ -56,7 +56,7 @@ def tile_list_moment_steps_listed_spread_kernel(tc, xf, ra, gt, rb, gk, bn, offs
         nc.sync.dma_start(g_tab[1][:], gt[P : 2 * P, :])
         nc.sync.dma_start(gk_col[:], gk.rearrange("(p h) o -> p (h o)", h=HALVES))
 
-        zero = keep.tile([P, 1], F32, name="zero")
+        zero = reused([P, 1], F32, "zero", "d")
         nc.gpsimd.memset(zero[:], 0.0)
         ident = keep.tile([P, P], F32, name="ident")
         make_identity(nc, ident[:])
@@ -64,8 +64,8 @@ def tile_list_moment_steps_listed_spread_kernel(tc, xf, ra, gt, rb, gk, bn, offs
         def turn_bank():
             return psum.tile([P, PACK, P], F32, name="turn", tag="turn", bufs=3)
 
-        x_pick = [reused([P, LEAD + J], F32, "x_pick0", "x_pick0")]
-        nc.scalar.activation(x_pick[0][:, LEAD - 1 : LEAD], zero[:], ACT.Copy)
+        x_first = keep.tile([P, LEAD + PASS], F32, name="x_first")
+        nc.scalar.activation(x_first[:, LEAD - 1 : LEAD], zero[:], ACT.Copy)
 
         def gather(on_vector, dst, table, entries, first, count):
             window = table[:].indirect(entries[:, first // PER_COL : (first + count) // PER_COL])
@@ -74,22 +74,17 @@ def tile_list_moment_steps_listed_spread_kernel(tc, xf, ra, gt, rb, gk, bn, offs
             else:
                 nc.scalar.activation(dst, window, ACT.Copy)
 
-        def x_gather(on_vector, h, a):
-            first = LEAD + a * PASS
-            gather(on_vector, x_pick[h][:, first : first + PASS], x_tab[h], x_list, a * PASS, PASS)
-
         u_codes = [keep.tile([P, PASSES * P], U32, name=f"u_codes{h}", align_bytes=64) for h in range(HALVES)]
         u_scales = [keep.tile([P, PASSES * P], U8, name=f"u_scales{h}", align_bytes=64) for h in range(HALVES)]
         g_codes = [keep.tile([P, PASSES * P], U32, name=f"g_codes{h}", align_bytes=64) for h in range(HALVES)]
         g_scales = [keep.tile([P, PASSES * P], U8, name=f"g_scales{h}", align_bytes=64) for h in range(HALVES)]
 
-        def x_step(h, a, step):
-            first = LEAD + a * PASS
+        def x_step(picked, first, step):
             nc.vector.scalar_tensor_tensor(
-                step[:].rearrange("p (t q) -> p q t", t=PACK),
-                x_pick[h][:, first - 1 : first - 1 + PASS].rearrange("p (q t) -> p q t", t=PACK),
+                step.rearrange("p (t q) -> p q t", t=PACK),
+                picked[:, first - 1 : first - 1 + PASS],
                 -0.6,
-                x_pick[h][:, first : first + PASS].rearrange("p (q t) -> p q t", t=PACK),
+                picked[:, first : first + PASS],
                 ALU.mult,
                 ALU.add,
             )
@@ -100,21 +95,17 @@ def tile_list_moment_steps_listed_spread_kernel(tc, xf, ra, gt, rb, gk, bn, offs
 
         def x_weigh(a, bank, u_bf):
             nc.vector.tensor_tensor(
-                u_bf[:].rearrange("p (k t) -> p k t", t=PACK),
+                u_bf.rearrange("p (k t) -> p k t", t=PACK),
                 bank[:].rearrange("p t k -> p k t"),
                 ra_col[:, a, :].unsqueeze(1).to_broadcast([P, P, PACK]),
                 ALU.mult,
             )
 
-        def x_quantise(h, a, u_bf):
-            cols = slice(a * P, (a + 1) * P)
-            nc.vector.quantize_mx(u_codes[h][:, cols].bitcast(E4M3), u_scales[h][:, cols], u_bf[:])
-
         def g_weigh(picked, weighed, a):
             nc.vector.tensor_tensor(
                 weighed.rearrange("p (u q e) -> p q u e", u=2, e=2),
-                picked.rearrange("p (q u e) -> p q u e", u=2, e=2),
-                rb_all[:, a * PASS : (a + 1) * PASS].rearrange("p (q u e) -> p q u e", u=2, e=2),
+                picked,
+                rb_all[:, a * PASS : (a + 1) * PASS],
                 ALU.mult,
             )
 
@@ -123,8 +114,6 @@ def tile_list_moment_steps_listed_spread_kernel(tc, xf, ra, gt, rb, gk, bn, offs
             for u in range(2):
                 nc.tensor.transpose(pairs_bank[:, u, :], words[:, u * P : (u + 1) * P], ident[:])
 
-        x_gather(True, 0, 0)
-        x_gather(False, 0, 1)
         rb_all = keep.tile([P, J], F32, name="rb_all")
         for a in range(PASSES):
             bank = turn_bank()
@@ -135,48 +124,49 @@ def tile_list_moment_steps_listed_spread_kernel(tc, xf, ra, gt, rb, gk, bn, offs
                 bank[:].rearrange("p t q -> p q t"),
             )
 
-        steps = [reused([P, PASS], F32, f"step0{a}", f"g0_pick{a}") for a in range(PASSES)]
-        banks = [x_step(0, a, steps[a]) for a in range(PASSES)]
-        u_bf = [reused([P, PASS], BF16, f"u_bf0{a}", f"early{a}") for a in range(PASSES)]
-        for a in range(PASSES):
-            x_weigh(a, banks[a], u_bf[a])
-        for a in range(PASSES):
-            x_quantise(0, a, u_bf[a])
-        g1_banks = [psum.tile([P, 2, 2, P], F32, name=f"g1_bank{a}") for a in range(PASSES)]
+        mixed_bank = psum.tile([P, PACK, P], F32, name="mixed_bank")
         for c in range(2):
-            nc.tensor.transpose(g1_banks[1][:, 1, c, :], bn_col[:, c : c + 1].to_broadcast([P, P]), ident[:])
-        x_pick.append(reused([P, LEAD + J], F32, "x_pick1", "first"))
-        nc.scalar.activation(x_pick[1][:, LEAD - 1 : LEAD], zero[:], ACT.Copy)
+            nc.tensor.transpose(mixed_bank[:, 2 + c, :], bn_col[:, c : c + 1].to_broadcast([P, P]), ident[:])
+        x_second = reused([P, LEAD + PASS], F32, "x_second", "a")
+        x_other = reused([P, LEAD + J], F32, "x_other", "b")
+        gather(True, x_first[:, LEAD:], x_tab[0], x_list, 0, PASS)
+        gather(False, x_second[:], x_tab[0], x_list, PASS - LEAD, LEAD + PASS)
+        nc.scalar.activation(x_other[:, LEAD - 1 : LEAD], zero[:], ACT.Copy)
         for a in range(PASSES):
-            x_gather(False, 1, a)
-        steps = [reused([P, PASS], F32, f"step1{a}", f"early{a}") for a in range(PASSES)]
-        banks = [x_step(1, a, steps[a]) for a in range(PASSES)]
-        u_bf = [reused([P, PASS], BF16, f"u_bf1{a}", f"late{a}") for a in range(PASSES)]
+            first = LEAD + a * PASS
+            gather(False, x_other[:, first : first + PASS], x_tab[1], x_list, a * PASS, PASS)
+        step00 = reused([P, PASS], F32, "step00", "c")
+        step01 = reused([P, PASS], F32, "step01", "e")
+        banks0 = [x_step(x_first, LEAD, step00[:]), x_step(x_second, LEAD, step01[:])]
+        u_bf0 = reused([P, J], BF16, "u_bf0", "a")
+        step1 = reused([P, J], F32, "step1", "e")
+        banks = []
         for a in range(PASSES):
-            x_weigh(a, banks[a], u_bf[a])
+            x_weigh(a, banks0[a], u_bf0[:, a * PASS : (a + 1) * PASS])
+            banks.append(x_step(x_other, LEAD + a * PASS, step1[:, a * PASS : (a + 1) * PASS]))
+        nc.vector.quantize_mx(u_codes[0][:].bitcast(E4M3), u_scales[0][:], u_bf0[:])
+        g0_pick = reused([P, J], F32, "g0_pick", "c")
         for a in range(PASSES):
-            x_quantise(1, a, u_bf[a])
-        g0_pick = [reused([P, PASS], F32, f"g0_pick{a}", f"g0_pick{a}") for a in range(PASSES)]
+            gather(False, g0_pick[:, a * PASS : (a + 1) * PASS], g_tab[0], g_list, a * PASS, PASS)
+        g1_pick = [reused([P, PASS], F32, "g1_pick0", "d"), reused([P, PASS], F32, "g1_pick1", "b")]
         for a in range(PASSES):
-            gather(False, g0_pick[a][:], g_tab[0], g_list, a * PASS, PASS)
-        g1_pick0 = reused([P, PASS], F32, "g1_pick0", "x_pick0")
-        gather(False, g1_pick0[:], g_tab[1], g_list, 0, PASS)
-        g0_bf = reused([P, J], BF16, "g0_bf", "late0")
-        g_weigh(g0_pick[0][:], g0_bf[:, 0:PASS], 0)
-        g1_pick1 = reused([P, PASS], F32, "g1_pick1", "late1")
-        quarter = PASS // 2
-        gather(False, g1_pick1[:, quarter:PASS], g_tab[1], g_list, PASS + quarter, quarter)
-        gather(True, g1_pick1[:, 0:quarter], g_tab[1], g_list, PASS, quarter)
-        g_weigh(g0_pick[1][:], g0_bf[:, PASS:J], 1)
+            gather(False, g1_pick[a][:], g_tab[1], g_list, a * PASS, PASS)
+        g0_bf = reused([P, J], BF16, "g0_bf", "a")
+        u_bf1 = keep.tile([P, J], BF16, name="u_bf1", align_bytes=64)
+        for a in range(PASSES):
+            x_weigh(a, banks[a], u_bf1[:, a * PASS : (a + 1) * PASS])
+            g_weigh(g0_pick[:, a * PASS : (a + 1) * PASS], g0_bf[:, a * PASS : (a + 1) * PASS], a)
         g0_bank = psum.tile([P, PASSES, 2, P], F32, name="g0_bank")
         for a in range(PASSES):
             g_turn(g0_bf[:, a * PASS : (a + 1) * PASS], g0_bank[:, a])
-        g1_bf0 = reused([P, PASS], BF16, "g1_bf0", "g0_pick0")
-        g_weigh(g1_pick0[:], g1_bf0[:], 0)
-        g_turn(g1_bf0[:], g1_banks[0][:, 0])
-        g1_bf1 = keep.tile([P, PASS], BF16, name="g1_bf1")
-        g_weigh(g1_pick1[:], g1_bf1[:], 1)
-        g_turn(g1_bf1[:], g1_banks[1][:, 0])
+        last_bank = psum.tile([P, 2, P], F32, name="last_bank")
+        g1_banks = [mixed_bank[:, 0:2, :], last_bank[:]]
+        g1_bf = [reused([P, PASS], BF16, "g1_bf0", "e"), reused([P, PASS], BF16, "g1_bf1", "c")]
+        g_weigh(g1_pick[0][:], g1_bf[0][:], 0)
+        g_turn(g1_bf[0][:], g1_banks[0])
+        nc.vector.quantize_mx(u_codes[1][:].bitcast(E4M3), u_scales[1][:], u_bf1[:])
+        g_weigh(g1_pick[1][:], g1_bf[1][:], 1)
+        g_turn(g1_bf[1][:], g1_banks[1])
 
         g0_in = keep.tile([P, PASSES * PASS], BF16, name="g0_in", align_bytes=64)
         nc.scalar.copy(
@@ -187,10 +177,10 @@ def tile_list_moment_steps_listed_spread_kernel(tc, xf, ra, gt, rb, gk, bn, offs
         for a in range(PASSES):
             nc.scalar.copy(
                 g1_in[a][:].bitcast(F32).rearrange("p (n u) -> p n u", u=2),
-                g1_banks[a][:, 0].rearrange("p u n -> p n u"),
+                g1_banks[a].rearrange("p u n -> p n u"),
             )
         bn_all = keep.tile([P, N], F32, name="bn_all")
-        nc.scalar.copy(bn_all[:].rearrange("p (q c) -> p q c", c=2), g1_banks[1][:, 1].rearrange("p c q -> p q c"))
+        nc.scalar.copy(bn_all[:].rearrange("p (q c) -> p q c", c=2), mixed_bank[:, 2:4, :].rearrange("p c q -> p q c"))
         nc.vector.quantize_mx(g_codes[0][:].bitcast(E5M2), g_scales[0][:], g0_in[:])
         for a in range(PASSES):
             cols = slice(a * P, (a + 1) * P)
@@ -233,8 +223,10 @@ def tile_list_moment_steps_listed_spread_kernel(tc, xf, ra, gt, rb, gk, bn, offs
             nc.vector.tensor_scalar(dev[h][:], wb[h][:], float(N), row_sum[:, h : h + 1], ALU.mult, ALU.subtract)
         den = keep.tile([P, HALVES], F32, name="den")
         inv = keep.tile([P, HALVES], F32, name="inv")
-        nc.vector.tensor_scalar(den[:], abs_sum[:], 1.0 / N, 2.0 * N, ALU.mult, ALU.add)
-        nc.vector.reciprocal(inv[:], den[:])
+        for h in range(HALVES):
+            nc.vector.tensor_scalar(den[:, h : h + 1], abs_sum[:, h : h + 1], 1.0 / N, 2.0 * N, ALU.mult, ALU.add)
+        for h in range(HALVES):
+            nc.vector.reciprocal(inv[:, h : h + 1], den[:, h : h + 1])
         for h in range(HALVES):
             y = keep.tile([P, N], F32, name=f"y{h}")
             nc.vector.tensor_scalar(y[:], dev[h][:], inv[:, h : h + 1], gk_col[:, h : h + 1], ALU.mult, ALU.mult)

@@ -81,7 +81,7 @@ def tile_list_moment_steps_listed_spread_kernel(tc, xf, ra, gt, rb, gk, bn, offs
 
         def x_step(picked, first, step):
             nc.vector.scalar_tensor_tensor(
-                step.rearrange("p (t q) -> p q t", t=PACK),
+                step,
                 picked[:, first - 1 : first - 1 + PASS],
                 -0.6,
                 picked[:, first : first + PASS],
@@ -90,7 +90,7 @@ def tile_list_moment_steps_listed_spread_kernel(tc, xf, ra, gt, rb, gk, bn, offs
             )
             bank = turn_bank()
             for t in range(PACK):
-                nc.tensor.transpose(bank[:, t, :], step[:, t * P : (t + 1) * P], ident[:])
+                nc.tensor.transpose(bank[:, t, :], step[:, t:PASS:PACK], ident[:])
             return bank
 
         def x_weigh(a, bank, u_bf):
@@ -103,7 +103,7 @@ def tile_list_moment_steps_listed_spread_kernel(tc, xf, ra, gt, rb, gk, bn, offs
 
         def g_weigh(picked, weighed, a):
             nc.vector.tensor_tensor(
-                weighed.rearrange("p (u q e) -> p q u e", u=2, e=2),
+                weighed,
                 picked,
                 rb_all[:, a * PASS : (a + 1) * PASS],
                 ALU.mult,
@@ -112,7 +112,7 @@ def tile_list_moment_steps_listed_spread_kernel(tc, xf, ra, gt, rb, gk, bn, offs
         def g_turn(weighed, pairs_bank):
             words = weighed.bitcast(F32)
             for u in range(2):
-                nc.tensor.transpose(pairs_bank[:, u, :], words[:, u * P : (u + 1) * P], ident[:])
+                nc.tensor.transpose(pairs_bank[:, u, :], words[:, u : 2 * P : 2], ident[:])
 
         rb_all = keep.tile([P, J], F32, name="rb_all")
         for a in range(PASSES):

@@ -40,29 +40,29 @@ def tile_list_moment_steps_listed_spread_kernel(tc, xf, ra, gt, rb, gk, bn, offs
         g_tab = [keep.tile([P, T], F32, name=f"g_tab{h}") for h in range(HALVES)]
         ra_col = keep.tile([P, PASSES, PACK], F32, name="ra_col")
         rb_col = reused([P, PASSES, PACK], F32, "rb_col", "a")
-        bn_col = reused([P, 2], F32, "bn_col", "b")
+        bn_col = keep.tile([P, 2], F32, name="bn_col")
         gk_col = keep.tile([P, HALVES], F32, name="gk_col")
 
         xf_rows = xf.rearrange("(p h) t -> p h t", h=HALVES)
         out_rows = out.rearrange("(p h) n -> p h n", h=HALVES)
-        nc.sync.dma_start(rb_col[:], rb.rearrange("o (a p t) -> p (o a) t", p=P, t=PACK))
+        nc.sync.dma_start(rb_col[:], rb.rearrange("o (p b t) -> p (o b) t", p=P, t=PACK))
         nc.sync.dma_start(x_tab[0][:], xf_rows[:, 0, :])
         nc.sync.dma_start(x_list[:], offs)
-        nc.sync.dma_start(ra_col[:], ra.rearrange("o (a p t) -> p (o a) t", p=P, t=PACK))
-        nc.sync.dma_start(bn_col[:], bn.rearrange("o (p c) -> p (o c)", c=2))
         nc.sync.dma_start(x_tab[1][:], xf_rows[:, 1, :])
+        nc.sync.dma_start(ra_col[:], ra.rearrange("o (a p t) -> p (o a) t", p=P, t=PACK))
         nc.sync.dma_start(g_list[:], offs2)
         nc.sync.dma_start(g_tab[0][:], gt[0:P, :])
         nc.sync.dma_start(g_tab[1][:], gt[P : 2 * P, :])
+        nc.sync.dma_start(bn_col[:], bn.rearrange("o (p c) -> p (o c)", c=2))
         nc.sync.dma_start(gk_col[:], gk.rearrange("(p h) o -> p (h o)", h=HALVES))
 
-        zero = reused([P, 1], F32, "zero", "d")
+        zero = keep.tile([P, 1], F32, name="zero")
         nc.gpsimd.memset(zero[:], 0.0)
         ident = keep.tile([P, P], F32, name="ident")
         make_identity(nc, ident[:])
 
-        def turn_bank():
-            return psum.tile([P, PACK, P], F32, name="turn", tag="turn", bufs=3)
+        def turn_bank(which):
+            return psum.tile([P, PACK, P], F32, name="turn", tag=f"turn{which}")
 
         x_first = keep.tile([P, LEAD + PASS], F32, name="x_first")
         nc.scalar.activation(x_first[:, LEAD - 1 : LEAD], zero[:], ACT.Copy)
@@ -79,7 +79,7 @@ def tile_list_moment_steps_listed_spread_kernel(tc, xf, ra, gt, rb, gk, bn, offs
         g_codes = [keep.tile([P, PASSES * P], U32, name=f"g_codes{h}", align_bytes=64) for h in range(HALVES)]
         g_scales = [keep.tile([P, PASSES * P], U8, name=f"g_scales{h}", align_bytes=64) for h in range(HALVES)]
 
-        def x_step(picked, first, step):
+        def x_step(picked, first, step, which):
             nc.vector.scalar_tensor_tensor(
                 step,
                 picked[:, first - 1 : first - 1 + PASS],
@@ -88,7 +88,7 @@ def tile_list_moment_steps_listed_spread_kernel(tc, xf, ra, gt, rb, gk, bn, offs
                 ALU.mult,
                 ALU.add,
             )
-            bank = turn_bank()
+            bank = turn_bank(which)
             for t in range(PACK):
                 nc.tensor.transpose(bank[:, t, :], step[:, t:PASS:PACK], ident[:])
             return bank
@@ -101,11 +101,11 @@ def tile_list_moment_steps_listed_spread_kernel(tc, xf, ra, gt, rb, gk, bn, offs
                 ALU.mult,
             )
 
-        def g_weigh(picked, weighed, a):
+        def g_weigh(picked, weighed, first, count):
             nc.vector.tensor_tensor(
                 weighed,
                 picked,
-                rb_all[:, a * PASS : (a + 1) * PASS],
+                rb_all[:, first : first + count],
                 ALU.mult,
             )
 
@@ -115,57 +115,65 @@ def tile_list_moment_steps_listed_spread_kernel(tc, xf, ra, gt, rb, gk, bn, offs
                 nc.tensor.transpose(pairs_bank[:, u, :], words[:, u : 2 * P : 2], ident[:])
 
         rb_all = keep.tile([P, J], F32, name="rb_all")
+        rb_banks = [turn_bank(a) for a in range(PASSES)]
         for a in range(PASSES):
-            bank = turn_bank()
             for t in range(PACK):
-                nc.tensor.transpose(bank[:, t, :], rb_col[:, a, t : t + 1].to_broadcast([P, P]), ident[:])
+                nc.tensor.transpose(rb_banks[a][:, t, :], rb_col[:, a, t : t + 1].to_broadcast([P, P]), ident[:])
+
+        def rb_out(a):
             nc.scalar.copy(
-                rb_all[:, a * PASS : (a + 1) * PASS].rearrange("p (q t) -> p q t", t=PACK),
-                bank[:].rearrange("p t q -> p q t"),
+                rb_all[:].rearrange("p (q b t) -> p b q t", b=2, t=PACK)[:, a],
+                rb_banks[a][:].rearrange("p t q -> p q t"),
             )
 
         mixed_bank = psum.tile([P, PACK, P], F32, name="mixed_bank")
-        for c in range(2):
-            nc.tensor.transpose(mixed_bank[:, 2 + c, :], bn_col[:, c : c + 1].to_broadcast([P, P]), ident[:])
+        half = PASS // 2
+        rb_out(0)
         x_second = reused([P, LEAD + PASS], F32, "x_second", "a")
-        x_other = reused([P, LEAD + J], F32, "x_other", "b")
         gather(True, x_first[:, LEAD:], x_tab[0], x_list, 0, PASS)
         gather(False, x_second[:], x_tab[0], x_list, PASS - LEAD, LEAD + PASS)
+        rb_out(1)
+        step00 = keep.tile([P, PASS], F32, name="step00")
+        step01 = reused([P, PASS], F32, "step01", "c")
+        banks0 = [x_step(x_first, LEAD, step00[:], 1), x_step(x_second, LEAD, step01[:], 0)]
+        x_other = reused([P, LEAD + J], F32, "x_other", "a")
+        gather(True, x_other[:, LEAD : LEAD + half], x_tab[1], x_list, 0, half)
+        gather(False, x_other[:, LEAD + half : LEAD + PASS], x_tab[1], x_list, half, half)
         nc.scalar.activation(x_other[:, LEAD - 1 : LEAD], zero[:], ACT.Copy)
-        for a in range(PASSES):
-            first = LEAD + a * PASS
-            gather(False, x_other[:, first : first + PASS], x_tab[1], x_list, a * PASS, PASS)
-        step00 = reused([P, PASS], F32, "step00", "c")
-        step01 = reused([P, PASS], F32, "step01", "e")
-        banks0 = [x_step(x_first, LEAD, step00[:]), x_step(x_second, LEAD, step01[:])]
-        u_bf0 = reused([P, J], BF16, "u_bf0", "a")
+        gather(False, x_other[:, LEAD + PASS :], x_tab[1], x_list, PASS, PASS)
+        u_bf0 = reused([P, J], BF16, "u_bf0", "b")
         step1 = reused([P, J], F32, "step1", "e")
         banks = []
         for a in range(PASSES):
             x_weigh(a, banks0[a], u_bf0[:, a * PASS : (a + 1) * PASS])
-            banks.append(x_step(x_other, LEAD + a * PASS, step1[:, a * PASS : (a + 1) * PASS]))
+            banks.append(x_step(x_other, LEAD + a * PASS, step1[:, a * PASS : (a + 1) * PASS], 2 - a))
         nc.vector.quantize_mx(u_codes[0][:].bitcast(E4M3), u_scales[0][:], u_bf0[:])
         g0_pick = reused([P, J], F32, "g0_pick", "c")
         for a in range(PASSES):
             gather(False, g0_pick[:, a * PASS : (a + 1) * PASS], g_tab[0], g_list, a * PASS, PASS)
-        g1_pick = [reused([P, PASS], F32, "g1_pick0", "d"), reused([P, PASS], F32, "g1_pick1", "b")]
-        for a in range(PASSES):
-            gather(False, g1_pick[a][:], g_tab[1], g_list, a * PASS, PASS)
-        g0_bf = reused([P, J], BF16, "g0_bf", "a")
+        g1_pick = [reused([P, PASS], F32, "g1_pick0", "a"), reused([P, PASS], F32, "g1_pick1", "b")]
+        gather(False, g1_pick[0][:], g_tab[1], g_list, 0, PASS)
+        pieces = ((0, PASS - P), (PASS - P, P))
+        for first, count in pieces:
+            gather(False, g1_pick[1][:, first : first + count], g_tab[1], g_list, PASS + first, count)
+        g0_bf = keep.tile([P, J], BF16, name="g0_bf")
         u_bf1 = keep.tile([P, J], BF16, name="u_bf1", align_bytes=64)
         for a in range(PASSES):
             x_weigh(a, banks[a], u_bf1[:, a * PASS : (a + 1) * PASS])
-            g_weigh(g0_pick[:, a * PASS : (a + 1) * PASS], g0_bf[:, a * PASS : (a + 1) * PASS], a)
+            g_weigh(g0_pick[:, a * PASS : (a + 1) * PASS], g0_bf[:, a * PASS : (a + 1) * PASS], a * PASS, PASS)
         g0_bank = psum.tile([P, PASSES, 2, P], F32, name="g0_bank")
         for a in range(PASSES):
             g_turn(g0_bf[:, a * PASS : (a + 1) * PASS], g0_bank[:, a])
         last_bank = psum.tile([P, 2, P], F32, name="last_bank")
         g1_banks = [mixed_bank[:, 0:2, :], last_bank[:]]
         g1_bf = [reused([P, PASS], BF16, "g1_bf0", "e"), reused([P, PASS], BF16, "g1_bf1", "c")]
-        g_weigh(g1_pick[0][:], g1_bf[0][:], 0)
+        g_weigh(g1_pick[0][:], g1_bf[0][:], 0, PASS)
         g_turn(g1_bf[0][:], g1_banks[0])
-        nc.vector.quantize_mx(u_codes[1][:].bitcast(E4M3), u_scales[1][:], u_bf1[:])
-        g_weigh(g1_pick[1][:], g1_bf[1][:], 1)
+        for c in range(2):
+            nc.tensor.transpose(mixed_bank[:, 2 + c, :], bn_col[:, c : c + 1].to_broadcast([P, P]), ident[:])
+        for first, count in pieces:
+            cols = slice(first, first + count)
+            g_weigh(g1_pick[1][:, cols], g1_bf[1][:, cols], PASS + first, count)
         g_turn(g1_bf[1][:], g1_banks[1])
 
         g0_in = keep.tile([P, PASSES * PASS], BF16, name="g0_in", align_bytes=64)
@@ -182,6 +190,7 @@ def tile_list_moment_steps_listed_spread_kernel(tc, xf, ra, gt, rb, gk, bn, offs
         bn_all = keep.tile([P, N], F32, name="bn_all")
         nc.scalar.copy(bn_all[:].rearrange("p (q c) -> p q c", c=2), mixed_bank[:, 2:4, :].rearrange("p c q -> p q c"))
         nc.vector.quantize_mx(g_codes[0][:].bitcast(E5M2), g_scales[0][:], g0_in[:])
+        nc.vector.quantize_mx(u_codes[1][:].bitcast(E4M3), u_scales[1][:], u_bf1[:])
         for a in range(PASSES):
             cols = slice(a * P, (a + 1) * P)
             nc.vector.quantize_mx(g_codes[1][:, cols].bitcast(E5M2), g_scales[1][:, cols], g1_in[a][:])

from contextlib import ExitStack

import concourse.mybir as mybir
from concourse.masks import make_identity

K, J, N, T = 256, 1024, 256, 2048
FLOPS = 2 * K * J * N

F32 = mybir.dt.float32
BF16 = mybir.dt.bfloat16
U32 = mybir.dt.uint32
U16 = mybir.dt.uint16
U8 = mybir.dt.uint8
E4M3 = mybir.dt.float8_e4m3fn_x4
E5M2 = mybir.dt.float8_e5m2_x4
ALU = mybir.AluOpType
ACT = mybir.ActivationFunctionType

P = 128
PACK = 4
PASS = P * PACK
PASSES = J // PASS
HALVES = 2
PER_COL = 16
LEAD = 2 * PER_COL


def tile_list_moment_steps_listed_spread_kernel(tc, xf, ra, gt, rb, gk, bn, offs, offs2, out):
    nc = tc.nc
    with ExitStack() as ctx:
        keep = ctx.enter_context(tc.tile_pool(name="keep", bufs=1))
        psum = ctx.enter_context(tc.psum_pool(name="psum", bufs=1))

        def reused(shape, dtype, name, tag):
            return keep.tile(shape, dtype, name=name, tag=tag, align_bytes=64)

        x_list = keep.tile([P, J // PER_COL], U16, name="x_list")
        g_list = keep.tile([P, J // PER_COL], U16, name="g_list")
        x_tab = [keep.tile([P, T], F32, name=f"x_tab{h}") for h in range(HALVES)]
        g_tab = [keep.tile([P, T], F32, name=f"g_tab{h}") for h in range(HALVES)]
        ra_col = keep.tile([P, PASSES, PACK], F32, name="ra_col")
        rb_col = reused([P, PASSES, PACK], F32, "rb_col", "a")
        bn_col = keep.tile([P, 2], F32, name="bn_col")
        gk_col = keep.tile([P, HALVES], F32, name="gk_col")

        xf_rows = xf.rearrange("(p h) t -> p h t", h=HALVES)
        out_rows = out.rearrange("(p h) n -> p h n", h=HALVES)
        nc.sync.dma_start(rb_col[:], rb.rearrange("o (p b t) -> p (o b) t", p=P, t=PACK))
        nc.sync.dma_start(x_tab[0][:], xf_rows[:, 0, :])
        nc.sync.dma_start(x_list[:], offs)
        nc.sync.dma_start(x_tab[1][:], xf_rows[:, 1, :])
        nc.sync.dma_start(ra_col[:], ra.rearrange("o (a p t) -> p (o a) t", p=P, t=PACK))
        nc.sync.dma_start(g_list[:], offs2)
        nc.sync.dma_start(g_tab[0][:], gt[0:P, :])
        nc.sync.dma_start(g_tab[1][:], gt[P : 2 * P, :])
        nc.sync.dma_start(bn_col[:], bn.rearrange("o (p c) -> p (o c)", c=2))
        nc.sync.dma_start(gk_col[:], gk.rearrange("(p h) o -> p (h o)", h=HALVES))

        zero = keep.tile([P, 1], F32, name="zero")
        nc.gpsimd.memset(zero[:], 0.0)
        ident = keep.tile([P, P], F32, name="ident")
        make_identity(nc, ident[:])

        def turn_bank(which):
            return psum.tile([P, PACK, P], F32, name="turn", tag=f"turn{which}")

        x_first = keep.tile([P, LEAD + PASS], F32, name="x_first")
        nc.scalar.activation(x_first[:, LEAD - 1 : LEAD], zero[:], ACT.Copy)

        def gather(on_vector, dst, table, entries, first, count):
            window = table[:].indirect(entries[:, first // PER_COL : (first + count) // PER_COL])
            if on_vector:
                nc.vector.tensor_copy(dst, window)
            else:
                nc.scalar.activation(dst, window, ACT.Copy)

        u_codes = [keep.tile([P, PASSES * P], U32, name=f"u_codes{h}", align_bytes=64) for h in range(HALVES)]
        u_scales = [keep.tile([P, PASSES * P], U8, name=f"u_scales{h}", align_bytes=64) for h in range(HALVES)]
        g_codes = [keep.tile([P, PASSES * P], U32, name=f"g_codes{h}", align_bytes=64) for h in range(HALVES)]
        g_scales = [keep.tile([P, PASSES * P], U8, name=f"g_scales{h}", align_bytes=64) for h in range(HALVES)]

        def x_step(picked, first, step, which):
            nc.vector.scalar_tensor_tensor(
                step,
                picked[:, first - 1 : first - 1 + PASS],
                -0.6,
                picked[:, first : first + PASS],
                ALU.mult,
                ALU.add,
            )
            bank = turn_bank(which)
            for t in range(PACK):
                nc.tensor.transpose(bank[:, t, :], step[:, t:PASS:PACK], ident[:])
            return bank

        def x_weigh(a, bank, u_bf):
            nc.vector.tensor_tensor(
                u_bf.rearrange("p (k t) -> p k t", t=PACK),
                bank[:].rearrange("p t k -> p k t"),
                ra_col[:, a, :].unsqueeze(1).to_broadcast([P, P, PACK]),
                ALU.mult,
            )

        def g_weigh(picked, weighed, first, count):
            nc.vector.tensor_tensor(
                weighed,
                picked,
                rb_all[:, first : first + count],
                ALU.mult,
            )

        def g_turn(weighed, pairs_bank):
            words = weighed.bitcast(F32)
            for u in range(2):
                nc.tensor.transpose(pairs_bank[:, u, :], words[:, u : 2 * P : 2], ident[:])

        rb_all = keep.tile([P, J], F32, name="rb_all")
        rb_banks = [turn_bank(a) for a in range(PASSES)]
        for a in range(PASSES):
            for t in range(PACK):
                nc.tensor.transpose(rb_banks[a][:, t, :], rb_col[:, a, t : t + 1].to_broadcast([P, P]), ident[:])

        def rb_out(a):
            nc.scalar.copy(
                rb_all[:].rearrange("p (q b t) -> p b q t", b=2, t=PACK)[:, a],
                rb_banks[a][:].rearrange("p t q -> p q t"),
            )

        mixed_bank = psum.tile([P, PACK, P], F32, name="mixed_bank")
        half = PASS // 2
        rb_out(0)
        x_second = reused([P, LEAD + PASS], F32, "x_second", "a")
        gather(True, x_first[:, LEAD:], x_tab[0], x_list, 0, PASS)
        gather(False, x_second[:], x_tab[0], x_list, PASS - LEAD, LEAD + PASS)
        rb_out(1)
        step00 = keep.tile([P, PASS], F32, name="step00")
        step01 = reused([P, PASS], F32, "step01", "c")
        banks0 = [x_step(x_first, LEAD, step00[:], 1), x_step(x_second, LEAD, step01[:], 0)]
        x_other = reused([P, LEAD + J], F32, "x_other", "a")
        gather(True, x_other[:, LEAD : LEAD + half], x_tab[1], x_list, 0, half)
        gather(False, x_other[:, LEAD + half : LEAD + PASS], x_tab[1], x_list, half, half)
        nc.scalar.activation(x_other[:, LEAD - 1 : LEAD], zero[:], ACT.Copy)
        gather(False, x_other[:, LEAD + PASS :], x_tab[1], x_list, PASS, PASS)
        u_bf0 = reused([P, J], BF16, "u_bf0", "b")
        step1 = reused([P, J], F32, "step1", "e")
        banks = []
        for a in range(PASSES):
            x_weigh(a, banks0[a], u_bf0[:, a * PASS : (a + 1) * PASS])
            banks.append(x_step(x_other, LEAD + a * PASS, step1[:, a * PASS : (a + 1) * PASS], 2 - a))
        nc.vector.quantize_mx(u_codes[0][:].bitcast(E4M3), u_scales[0][:], u_bf0[:])
        g0_pick = reused([P, J], F32, "g0_pick", "c")
        for a in range(PASSES):
            gather(False, g0_pick[:, a * PASS : (a + 1) * PASS], g_tab[0], g_list, a * PASS, PASS)
        g1_pick = [reused([P, PASS], F32, "g1_pick0", "a"), reused([P, PASS], F32, "g1_pick1", "b")]
        gather(False, g1_pick[0][:], g_tab[1], g_list, 0, PASS)
        pieces = ((0, PASS - P), (PASS - P, P))
        for first, count in pieces:
            gather(False, g1_pick[1][:, first : first + count], g_tab[1], g_list, PASS + first, count)
        g0_bf = keep.tile([P, J], BF16, name="g0_bf")
        u_bf1 = keep.tile([P, J], BF16, name="u_bf1", align_bytes=64)
        for a in range(PASSES):
            x_weigh(a, banks[a], u_bf1[:, a * PASS : (a + 1) * PASS])
            g_weigh(g0_pick[:, a * PASS : (a + 1) * PASS], g0_bf[:, a * PASS : (a + 1) * PASS], a * PASS, PASS)
        g0_bank = psum.tile([P, PASSES, 2, P], F32, name="g0_bank")
        for a in range(PASSES):
            g_turn(g0_bf[:, a * PASS : (a + 1) * PASS], g0_bank[:, a])
        last_bank = psum.tile([P, 2, P], F32, name="last_bank")
        g1_banks = [mixed_bank[:, 0:2, :], last_bank[:]]
        g1_bf = [reused([P, PASS], BF16, "g1_bf0", "e"), reused([P, PASS], BF16, "g1_bf1", "c")]
        g_weigh(g1_pick[0][:], g1_bf[0][:], 0, PASS)
        g_turn(g1_bf[0][:], g1_banks[0])
        for c in range(2):
            nc.tensor.transpose(mixed_bank[:, 2 + c, :], bn_col[:, c : c + 1].to_broadcast([P, P]), ident[:])
        for first, count in pieces:
            cols = slice(first, first + count)
            g_weigh(g1_pick[1][:, cols], g1_bf[1][:, cols], PASS + first, count)
        g_turn(g1_bf[1][:], g1_banks[1])

        g0_in = keep.tile([P, PASSES * PASS], BF16, name="g0_in", align_bytes=64)
        nc.scalar.copy(
            g0_in[:].bitcast(F32).rearrange("p (a n u) -> p a n u", a=PASSES, u=2),
            g0_bank[:].rearrange("p a u n -> p a n u"),
        )
        g1_in = [keep.tile([P, PASS], BF16, name=f"g1_in{a}", align_bytes=64) for a in range(PASSES)]
        for a in range(PASSES):
            nc.scalar.copy(
                g1_in[a][:].bitcast(F32).rearrange("p (n u) -> p n u", u=2),
                g1_banks[a].rearrange("p u n -> p n u"),
            )
        bn_all = keep.tile([P, N], F32, name="bn_all")
        nc.scalar.copy(bn_all[:].rearrange("p (q c) -> p q c", c=2), mixed_bank[:, 2:4, :].rearrange("p c q -> p q c"))
        nc.vector.quantize_mx(g_codes[0][:].bitcast(E5M2), g_scales[0][:], g0_in[:])
        nc.vector.quantize_mx(u_codes[1][:].bitcast(E4M3), u_scales[1][:], u_bf1[:])
        for a in range(PASSES):
            cols = slice(a * P, (a + 1) * P)
            nc.vector.quantize_mx(g_codes[1][:, cols].bitcast(E5M2), g_scales[1][:, cols], g1_in[a][:])

        w = [psum.tile([P, N], F32, name=f"w{h}") for h in range(HALVES)]

        def product(h, c, a):
            cols = slice(a * P, (a + 1) * P)
            nc.tensor.matmul_mx(
                out=w[h][:, c * P : (c + 1) * P],
                lhsT=u_codes[h][:, cols].bitcast(E4M3),
                lhsT_scale=u_scales[h][:, cols],
                rhs=g_codes[c][:, cols].bitcast(E5M2),
                rhs_scale=g_scales[c][:, cols],
                start=(a == 0),
                stop=(a == PASSES - 1),
            )

        for h in range(HALVES):
            for a in range(PASSES):
                product(h, 0, a)
        for a in range(PASSES):
            for h in range(HALVES):
                product(h, 1, a)

        row_sum = keep.tile([P, HALVES], F32, name="row_sum")
        abs_sum = keep.tile([P, HALVES], F32, name="abs_sum")
        wb = [keep.tile([P, N], F32, name=f"wb{h}") for h in range(HALVES)]
        for h in range(HALVES):
            nc.vector.scalar_tensor_tensor(
                wb[h][:], w[h][:], 1.0, bn_all[:], ALU.mult, ALU.add, accum_out=row_sum[:, h : h + 1]
            )
        dev = [keep.tile([P, N], F32, name=f"dev{h}") for h in range(HALVES)]
        for h in range(HALVES):
            size = keep.tile([P, N], F32, name=f"size{h}")
            nc.scalar.activation(
                size[:], wb[h][:], ACT.Abs, bias=row_sum[:, h : h + 1], scale=-float(N), accum_out=abs_sum[:, h : h + 1]
            )
            nc.vector.tensor_scalar(dev[h][:], wb[h][:], float(N), row_sum[:, h : h + 1], ALU.mult, ALU.subtract)
        den = keep.tile([P, HALVES], F32, name="den")
        inv = keep.tile([P, HALVES], F32, name="inv")
        for h in range(HALVES):
            nc.vector.tensor_scalar(den[:, h : h + 1], abs_sum[:, h : h + 1], 1.0 / N, 2.0 * N, ALU.mult, ALU.add)
        for h in range(HALVES):
            nc.vector.reciprocal(inv[:, h : h + 1], den[:, h : h + 1])
        for h in range(HALVES):
            y = keep.tile([P, N], F32, name=f"y{h}")
            nc.vector.tensor_scalar(y[:], dev[h][:], inv[:, h : h + 1], gk_col[:, h : h + 1], ALU.mult, ALU.mult)
            queue = nc.sync if h == 0 else nc.scalar
            queue.dma_start(out_rows[:, h, :], y[:])
